import numpy as np
import ml_dtypes


def mxq(x, axis, fmt="e4m3"):
    dtype, down = {"e4m3": (ml_dtypes.float8_e4m3fn, 7), "e5m2": (ml_dtypes.float8_e5m2, 14)}[fmt]
    v = np.moveaxis(np.asarray(x, np.float32).astype(ml_dtypes.bfloat16).astype(np.float64), axis, -1)
    blocks = v.reshape(v.shape[:-1] + (-1, 32))
    amax = np.abs(blocks).max(-1, keepdims=True)
    byte = np.maximum(np.where(amax > 0, np.frexp(amax)[1] - 1 + 127, 0) - down, 1)
    scale = np.exp2(byte - 127.0)
    codes = (blocks / scale).astype(np.float32).astype(dtype).astype(np.float64)
    return np.moveaxis((codes * scale).reshape(v.shape), -1, axis)


WIDE = False


def mx_kscale(k):
    if not WIDE:
        return np.ones(k)
    levels = np.array([10, -10, 5, -5, 0])
    if k % 512:
        return np.exp2(np.random.permutation(np.resize(levels, k // 32))).repeat(32)
    a = np.empty((k // 512, 16))
    for p in range(k // 512):
        a[p, :8] = np.random.permutation(np.resize(levels, 8))
        for g in range(8):
            far = levels[np.abs(levels - a[p, g]) >= 10]
            a[p, g + 8] = far[np.random.randint(len(far))]
    return np.exp2(a.ravel()).repeat(32)


def f64(x):
    return np.asarray(x).astype(np.float64)


def striped(idx):
    return np.tile(idx.reshape(-1, 16).T, (8, 1)).astype(np.uint16)


def unstriped(offs):
    return offs[:16].T.reshape(-1).astype(np.int64)


def pack_weight(w):
    k, n = w.shape
    w = f64(np.asarray(w, np.float32).astype(ml_dtypes.bfloat16)).reshape(k // 32, 32, n)
    amax = np.abs(w).max(1)
    byte = np.clip(np.where(amax > 0, np.frexp(amax)[1] - 1 + 127 - 7, 1), 1, 254)
    scaled = (w * np.exp2(127.0 - byte)[:, None, :]).reshape(k, n).astype(np.float32)
    words = np.ascontiguousarray(scaled.reshape(k // 512, 128, 4, n).transpose(0, 1, 3, 2)).astype(ml_dtypes.float8_e4m3fn).view(np.uint8)
    return words, np.ascontiguousarray(byte.astype(np.uint8).reshape(k // 512, 16, n))


def unpack_weight(words, scales):
    g, p, n, _ = words.shape
    vals = np.ascontiguousarray(words).view(ml_dtypes.float8_e4m3fn).astype(np.float64) * np.repeat(np.exp2(scales.astype(np.float64) - 127.0), 8, axis=1)[..., None]
    return vals.transpose(0, 1, 3, 2).reshape(g * 512, n)


def planes(y):
    n, m = y.shape
    v = y.astype(np.float32).astype(ml_dtypes.bfloat16).astype(np.float64).reshape(n // 32, 32, m)
    top = np.abs(v).max(1)
    byte = np.clip(np.where(top > 0, np.frexp(top)[1] - 1 + 127 - 7, 1), 1, 254)
    codes = (v * np.exp2(127.0 - byte)[:, None, :]).reshape(n, m).astype(np.float32).astype(ml_dtypes.float8_e4m3fn).view(np.uint8)
    words = codes.reshape(n // 512, 128, 4, m).transpose(0, 1, 3, 2)
    return np.ascontiguousarray(words), np.ascontiguousarray(byte.astype(np.uint8).reshape(n // 512, 16, m))


def gelu(v):
    return 0.5 * v * (1.0 + np.tanh(np.sqrt(2.0 / np.pi) * (v + 0.044715 * v**3)))


K, T, S, H, N = 512, 1024, 512, 512, 512


def setup_inputs():
    n = np.random.standard_normal
    s = mx_kscale(K)[:, None]
    u = mx_kscale(H)
    packed_xT = pack_weight(n((K, T)) * s)
    packed_w2 = pack_weight(n((K, N)) / np.sqrt(K) / s)
    packed_w5 = pack_weight(n((H, N)) / np.sqrt(2 * H) / u[:, None])
    packed_w6 = pack_weight(n((H, N)) / np.sqrt(2 * H) / u[:, None])
    return {
        "x_words": packed_xT[0],
        "x_scales": packed_xT[1],
        "w1": (n((K, H)) / np.sqrt(K) / s * u).astype(np.float32),
        "w2_words": packed_w2[0],
        "w2_scales": packed_w2[1],
        "w3": (n((K, H)) / np.sqrt(2 * K) / s * u).astype(np.float32),
        "w4": (n((K, H)) / np.sqrt(2 * K) / s * u).astype(np.float32),
        "w5_words": packed_w5[0],
        "w5_scales": packed_w5[1],
        "w6_words": packed_w6[0],
        "w6_scales": packed_w6[1],
        "offs": striped(np.random.permutation(T)[:S]),
        "end": striped(np.random.permutation(T)[:S]),
    }


def reference(x_words, x_scales, w1, w2_words, w2_scales, w3, w4, w5_words, w5_scales, w6_words, w6_scales, offs, end):
    xq = unpack_weight(x_words, x_scales)[:, unstriped(offs)]
    y = mxq(f64(w1), 0, "e4m3").T @ xq
    x_end = unpack_weight(x_words, x_scales)[:, unstriped(end)]
    e = unpack_weight(w2_words, w2_scales).T @ x_end
    z = y * e
    g = gelu(mxq(f64(w3), 0, "e4m3").T @ xq + mxq(f64(w4), 0, "e4m3").T @ x_end)
    out_0 = unpack_weight(w5_words, w5_scales).T @ mxq(z, 0, "e4m3") + unpack_weight(w6_words, w6_scales).T @ mxq(g, 0, "e4m3")
    return (out_0,) + planes(out_0)

@@ -1,0 +1,223 @@
+from contextlib import ExitStack
+
+import concourse.mybir as mybir
+
+K, T, S, H, N = 512, 1024, 512, 512, 512
+FLOPS = 2 * S * (4 * K * H + 2 * H * N)
+
+F32 = mybir.dt.float32
+BF16 = mybir.dt.bfloat16
+I32 = mybir.dt.int32
+U32 = mybir.dt.uint32
+U16 = mybir.dt.uint16
+U8 = mybir.dt.uint8
+FP8X4 = mybir.dt.float8_e4m3fn_x4
+GELU = mybir.ActivationFunctionType.Gelu_apprx_tanh
+MULT = mybir.AluOpType.mult
+
+P = 128
+PACK = 4
+QUADS = 4
+SPANS = 128
+BLOCKS = S // SPANS
+HALF = H // 2
+
+
+def tile_picked_zspan_gelu_po_kernel(
+    tc, x_words, x_scales, w1, w2_words, w2_scales, w3, w4, w5_words, w5_scales, w6_words, w6_scales, offs, end,
+    out_0, out_1, out_2,
+):
+    nc = tc.nc
+    with ExitStack() as ctx:
+        keep = ctx.enter_context(tc.tile_pool(name="keep", bufs=1))
+        psum = ctx.enter_context(tc.psum_pool(name="psum", bufs=1))
+
+        def sb(name, shape, dtype, tag=None):
+            return keep.tile(shape, dtype, name=name, tag=tag or name, align_bytes=64)
+
+        def bank(index, name):
+            return psum.tile([P, PACK, SPANS], F32, name=name, tag="bank%d" % index)
+
+        def as_words(packed):
+            return packed[0].rearrange("p n t -> p (n t)").bitcast(I32)
+
+        def load_scale_rows(queue, plane, scales, first):
+            for q in range(QUADS):
+                queue.dma_start(
+                    out=plane[32 * q + first : 32 * q + first + 4, :].bitcast(I32),
+                    in_=scales[0, 4 * q : 4 * q + 4, :].bitcast(I32),
+                )
+
+        def load_half(name, w, half):
+            raw = sb(name, [P, PACK, HALF], F32)
+            nc.sync.dma_start(
+                out=raw[:], in_=w.rearrange("(p j) c -> p j c", j=PACK)[:, :, half * HALF : (half + 1) * HALF]
+            )
+            return raw
+
+        def round_half(copy, grouped, raw, half):
+            m = slice(half * P // 2, (half + 1) * P // 2)
+            copy(
+                out=grouped[:, :, m, :].rearrange("p t m j -> p m j t"),
+                in_=raw[:].rearrange("p j (m t) -> p m j t", t=PACK),
+            )
+
+        def quantise(codes, scales, values):
+            nc.vector.quantize_mx(out=codes.bitcast(FP8X4), scales=scales, in_=values)
+
+        def deal(name, src, dtype):
+            dealt = sb(name, [P, H], dtype)
+            nc.vector.tensor_copy(
+                out=dealt[:].rearrange("p (t m) -> p m t", t=PACK), in_=src[:].rearrange("p (m t) -> p m t", t=PACK)
+            )
+            return dealt
+
+        def product(acc, terms, cols):
+            for t in range(PACK):
+                rows = slice(t * P, (t + 1) * P)
+                for i, (w_codes, w_scales, a_codes, a_scales) in enumerate(terms):
+                    nc.tensor.matmul_mx(
+                        out=acc[:, t, :],
+                        lhsT=w_codes[:, rows].bitcast(FP8X4),
+                        lhsT_scale=w_scales[:, rows],
+                        rhs=a_codes[:, cols].bitcast(FP8X4),
+                        rhs_scale=a_scales[:, cols],
+                        start=(i == 0),
+                        stop=(i == len(terms) - 1),
+                    )
+
+        x_plane = sb("x_plane", [P, T], U8)
+        w2_plane = sb("w2_plane", [P, H], U8)
+        w56_plane = sb("w56_plane", [P, N], U8)
+        for plane in (x_plane, w2_plane, w56_plane):
+            nc.gpsimd.memset(plane[:].bitcast(I32), 0)
+        warm = sb("warm", [P, 2], F32)
+        nc.gpsimd.memset(warm[:, 0:1], 0.0)
+        nc.scalar.activation(out=warm[:, 1:2], in_=warm[:, 0:1], func=GELU)
+        end_list = sb("end_list", [P, S // 16], U16)
+        offs_list = sb("offs_list", [P, S // 16], U16)
+        x_table = sb("x_table", [P, T], I32)
+        w2_raw = sb("w2_raw", [P, H], I32)
+        w5_raw = sb("w5_raw", [P, N], I32)
+        w6_raw = sb("w6_raw", [P, N], I32)
+        load_scale_rows(nc.scalar, x_plane, x_scales, 0)
+        load_scale_rows(nc.gpsimd, w2_plane, w2_scales, 0)
+        load_scale_rows(nc.gpsimd, w56_plane, w5_scales, 0)
+        load_scale_rows(nc.gpsimd, w56_plane, w6_scales, 4)
+        nc.sync.dma_start(end_list[:], end)
+        nc.sync.dma_start(offs_list[:], offs)
+        nc.sync.dma_start(out=x_table[:], in_=as_words(x_words))
+        w1_raw = sb("w1_raw", [P, PACK, H], F32)
+        nc.sync.dma_start(out=w1_raw[:], in_=w1.rearrange("(p j) c -> p j c", j=PACK))
+        nc.sync.dma_start(out=w2_raw[:], in_=as_words(w2_words))
+        w3_raw = [load_half("w3_raw%d" % h, w3, h) for h in range(2)]
+        w4_raw = [load_half("w4_raw%d" % h, w4, h) for h in range(2)]
+        nc.sync.dma_start(out=w5_raw[:], in_=as_words(w5_words))
+        nc.sync.dma_start(out=w6_raw[:], in_=as_words(w6_words))
+        xe_scales = sb("xe_scales", [P, S], U8)
+        xs_scales = sb("xs_scales", [P, S], U8)
+        xe_codes = sb("xe_codes", [P, S], U32)
+        nc.vector.tensor_copy(xe_scales[:], x_plane[:].indirect(end_list[:]))
+        nc.vector.tensor_copy(xs_scales[:], x_plane[:].indirect(offs_list[:]))
+        nc.vector.tensor_copy(xe_codes[:], x_table[:].bitcast(U32).indirect(end_list[:]))
+
+        grouped = {n: sb("w%d_grouped" % n, [P, PACK, P, PACK], BF16) for n in (1, 3, 4)}
+        codes = {n: sb("w%d_codes" % n, [P, H], U32) for n in (1, 3, 4)}
+        scales = {n: sb("w%d_scales_q" % n, [P, H], U8) for n in (1, 3, 4)}
+
+        def quantise_weight(n):
+            quantise(codes[n][:], scales[n][:], grouped[n][:].rearrange("p t m j -> p (t m j)"))
+
+        def quantise_weight_by_tile(n):
+            for t in range(PACK):
+                rows = slice(t * P, (t + 1) * P)
+                quantise(codes[n][:, rows], scales[n][:, rows], grouped[n][:, t, :, :].rearrange("p m j -> p (m j)"))
+
+        blocks = [slice(b * SPANS, (b + 1) * SPANS) for b in range(BLOCKS)]
+        z_codes = sb("z_codes", [P, S], U32)
+        z_scales = sb("z_scales", [P, S], U8)
+        g_codes = sb("g_codes", [P, S], U32)
+        g_scales = sb("g_scales", [P, S], U8)
+        o_codes = sb("o_codes", [P, S], I32)
+        o_scales = sb("o_scales", [P, S], U8)
+        e_vals = {}
+        z_vals = {}
+        g_vals = [sb("g_vals%d" % b, [P, SPANS, PACK], BF16) for b in range(BLOCKS)]
+        o_vals = [sb("o_vals%d" % b, [P, PACK, SPANS], F32) for b in range(BLOCKS)]
+        o_round = [sb("o_round%d" % b, [P, SPANS, PACK], BF16) for b in range(BLOCKS)]
+        out_rows = out_0.rearrange("(p t) j -> p t j", t=PACK)
+        out_words = as_words(out_1)
+
+        def ends(b, bk, tag):
+            acc = bank(bk, "e_acc%d" % b)
+            product(acc, [(w2_codes, w2_dealt, xe_codes, xe_scales)], blocks[b])
+            e_vals[b] = sb("e_vals%d" % b, [P, SPANS, PACK], F32, tag)
+            nc.scalar.copy(out=e_vals[b][:], in_=acc[:].rearrange("p t n -> p n t"))
+
+        def additive(b, bk):
+            acc = bank(bk, "g_acc%d" % b)
+            product(acc, [(codes[3], scales[3], xs_codes, xs_scales), (codes[4], scales[4], xe_codes, xe_scales)], blocks[b])
+            nc.scalar.activation(out=g_vals[b][:], in_=acc[:].rearrange("p t n -> p n t"), func=GELU)
+            quantise(g_codes[:, blocks[b]], g_scales[:, blocks[b]], g_vals[b][:].rearrange("p n t -> p (n t)"))
+
+        def starts(b, bk, tag):
+            acc = bank(bk, "y_acc%d" % b)
+            product(acc, [(codes[1], scales[1], xs_codes, xs_scales)], blocks[b])
+            z_vals[b] = sb("z_vals%d" % b, [P, SPANS, PACK], BF16, tag)
+            nc.vector.tensor_tensor(z_vals[b][:], acc[:].rearrange("p t n -> p n t"), e_vals[b][:], MULT)
+
+        def quantise_z(b):
+            quantise(z_codes[:, blocks[b]], z_scales[:, blocks[b]], z_vals[b][:].rearrange("p n t -> p (n t)"))
+
+        def labels(b, bk, round_from_psum):
+            acc = bank(bk, "o_acc%d" % b)
+            product(acc, [(w5_codes, w56_dealt, z_codes, z_scales), (w6_codes, w56_dealt[4:P, :], g_codes, g_scales)], blocks[b])
+            if round_from_psum is not None:
+                round_from_psum(out=o_round[b][:], in_=acc[:].rearrange("p t n -> p n t"))
+            nc.scalar.copy(out=o_vals[b][:], in_=acc[:])
+            nc.sync.dma_start(out=out_rows[:, :, blocks[b]], in_=o_vals[b][:])
+            if round_from_psum is None:
+                nc.vector.tensor_copy(
+                    out=o_round[b][:].rearrange("p (c i) t -> p c t i", i=PACK),
+                    in_=o_vals[b][:].rearrange("p t (c i) -> p c t i", i=PACK),
+                )
+
+        def planes(b):
+            quantise(o_codes[:, blocks[b]], o_scales[:, blocks[b]], o_round[b][:].rearrange("p n t -> p (n t)"))
+            nc.sync.dma_start(out=out_words[:, blocks[b]], in_=o_codes[:, blocks[b]])
+        w2_dealt = deal("w2_dealt", w2_plane, U8)
+        w2_codes = deal("w2_codes", w2_raw, I32)
+        xs_codes = sb("xs_codes", [P, S], U32, "w2_raw")
+        nc.vector.tensor_copy(xs_codes[:], x_table[:].bitcast(U32).indirect(offs_list[:]))
+        nc.scalar.copy(
+            out=grouped[1][:].rearrange("p t m j -> p m j t"), in_=w1_raw[:].rearrange("p j (m t) -> p m j t", t=PACK)
+        )
+        quantise_weight(1)
+        for h in range(2):
+            round_half(nc.scalar.copy, grouped[3], w3_raw[h], h)
+        quantise_weight(3)
+        for b in range(BLOCKS):
+            ends(b, b, "w3_raw1" if b == 0 else None)
+        for h in range(2):
+            round_half(nc.vector.tensor_copy, grouped[4], w4_raw[h], h)
+        quantise_weight_by_tile(4)
+        w56_dealt = deal("w56_dealt", w56_plane, U8)
+        w5_codes = deal("w5_codes", w5_raw, I32)
+        w6_codes = deal("w6_codes", w6_raw, I32)
+        for b in range(BLOCKS):
+            starts(b, BLOCKS + b, "w4_grouped" if b == 1 else None)
+            if b > 0:
+                quantise_z(b - 1)
+        quantise_z(BLOCKS - 1)
+        rounders = [None, nc.scalar.copy, nc.scalar.copy, nc.vector.tensor_copy]
+        for b in range(BLOCKS):
+            additive(b, b)
+        for b in range(BLOCKS):
+            labels(b, BLOCKS + b, rounders[b])
+            if b > 0:
+                planes(b - 1)
+        planes(BLOCKS - 1)
+        for q in range(QUADS):
+            nc.sync.dma_start(
+                out=out_2[0, 4 * q : 4 * q + 4, :].bitcast(I32), in_=o_scales[32 * q : 32 * q + 4, :].bitcast(I32)
+            )

@@ -55,18 +55,22 @@ def tile_picked_zspan_gelu_po_kernel(
             )
             return raw
 
-        def round_half(copy, grouped, raw, half):
-            m = slice(half * P // 2, (half + 1) * P // 2)
+        def load_whole(name, w):
+            raw = sb(name, [P, PACK, H], F32)
+            nc.sync.dma_start(out=raw[:], in_=w.rearrange("(p j) c -> p j c", j=PACK))
+            return raw
+
+        def round_cols(copy, grouped, raw, first, count, base):
             copy(
-                out=grouped[:, :, m, :].rearrange("p t m j -> p m j t"),
-                in_=raw[:].rearrange("p j (m t) -> p m j t", t=PACK),
+                out=grouped[:, :, first : first + count, :].rearrange("p t m j -> p m j t"),
+                in_=raw[:].rearrange("p j (m t) -> p m j t", t=PACK)[:, first - base : first - base + count, :, :],
             )
 
         def quantise(codes, scales, values):
             nc.vector.quantize_mx(out=codes.bitcast(FP8X4), scales=scales, in_=values)
 
-        def deal(name, src, dtype):
-            dealt = sb(name, [P, H], dtype)
+        def deal(name, src, dtype, tag=None):
+            dealt = sb(name, [P, H], dtype, tag)
             nc.vector.tensor_copy(
                 out=dealt[:].rearrange("p (t m) -> p m t", t=PACK), in_=src[:].rearrange("p (m t) -> p m t", t=PACK)
             )
@@ -89,8 +93,9 @@ def tile_picked_zspan_gelu_po_kernel(
         x_plane = sb("x_plane", [P, T], U8)
         w2_plane = sb("w2_plane", [P, H], U8)
         w56_plane = sb("w56_plane", [P, N], U8)
-        for plane in (x_plane, w2_plane, w56_plane):
-            nc.gpsimd.memset(plane[:].bitcast(I32), 0)
+        nc.gpsimd.memset(x_plane[:].bitcast(I32), 0)
+        nc.vector.memset(w2_plane[:].bitcast(I32), 0)
+        nc.vector.memset(w56_plane[:].bitcast(I32), 0)
         warm = sb("warm", [P, 2], F32)
         nc.gpsimd.memset(warm[:, 0:1], 0.0)
         nc.scalar.activation(out=warm[:, 1:2], in_=warm[:, 0:1], func=GELU)
@@ -98,22 +103,21 @@ def tile_picked_zspan_gelu_po_kernel(
         offs_list = sb("offs_list", [P, S // 16], U16)
         x_table = sb("x_table", [P, T], I32)
         w2_raw = sb("w2_raw", [P, H], I32)
-        w5_raw = sb("w5_raw", [P, N], I32)
-        w6_raw = sb("w6_raw", [P, N], I32)
-        load_scale_rows(nc.scalar, x_plane, x_scales, 0)
-        load_scale_rows(nc.gpsimd, w2_plane, w2_scales, 0)
-        load_scale_rows(nc.gpsimd, w56_plane, w5_scales, 0)
-        load_scale_rows(nc.gpsimd, w56_plane, w6_scales, 4)
+        w56_raw = sb("w56_raw", [P, 2, N], I32)
         nc.sync.dma_start(end_list[:], end)
         nc.sync.dma_start(offs_list[:], offs)
+        load_scale_rows(nc.sync, x_plane, x_scales, 0)
         nc.sync.dma_start(out=x_table[:], in_=as_words(x_words))
-        w1_raw = sb("w1_raw", [P, PACK, H], F32)
-        nc.sync.dma_start(out=w1_raw[:], in_=w1.rearrange("(p j) c -> p j c", j=PACK))
+        w1_raw = load_whole("w1_raw", w1)
+        load_scale_rows(nc.sync, w2_plane, w2_scales, 0)
         nc.sync.dma_start(out=w2_raw[:], in_=as_words(w2_words))
-        w3_raw = [load_half("w3_raw%d" % h, w3, h) for h in range(2)]
-        w4_raw = [load_half("w4_raw%d" % h, w4, h) for h in range(2)]
-        nc.sync.dma_start(out=w5_raw[:], in_=as_words(w5_words))
-        nc.sync.dma_start(out=w6_raw[:], in_=as_words(w6_words))
+        w3_raw = load_whole("w3_raw", w3)
+        w4_raw = [load_half("w4_raw0", w4, 0)]
+        load_scale_rows(nc.sync, w56_plane, w5_scales, 0)
+        w4_raw.append(load_half("w4_raw1", w4, 1))
+        nc.sync.dma_start(out=w56_raw[:, 0, :], in_=as_words(w5_words))
+        nc.sync.dma_start(out=w56_raw[:, 1, :], in_=as_words(w6_words))
+        load_scale_rows(nc.sync, w56_plane, w6_scales, 4)
         xe_scales = sb("xe_scales", [P, S], U8)
         xs_scales = sb("xs_scales", [P, S], U8)
         xe_codes = sb("xe_codes", [P, S], U32)
@@ -121,9 +125,12 @@ def tile_picked_zspan_gelu_po_kernel(
         nc.vector.tensor_copy(xs_scales[:], x_plane[:].indirect(offs_list[:]))
         nc.vector.tensor_copy(xe_codes[:], x_table[:].bitcast(U32).indirect(end_list[:]))
 
-        grouped = {n: sb("w%d_grouped" % n, [P, PACK, P, PACK], BF16) for n in (1, 3, 4)}
-        codes = {n: sb("w%d_codes" % n, [P, H], U32) for n in (1, 3, 4)}
-        scales = {n: sb("w%d_scales_q" % n, [P, H], U8) for n in (1, 3, 4)}
+        grouped, codes, scales = {}, {}, {}
+
+        def new_weight(n, grouped_tag=None, codes_tag=None, scales_tag=None):
+            grouped[n] = sb("w%d_grouped" % n, [P, PACK, P, PACK], BF16, grouped_tag)
+            codes[n] = sb("w%d_codes" % n, [P, H], U32, codes_tag)
+            scales[n] = sb("w%d_scales_q" % n, [P, H], U8, scales_tag)
 
         def quantise_weight(n):
             quantise(codes[n][:], scales[n][:], grouped[n][:].rearrange("p t m j -> p (t m j)"))
@@ -134,15 +141,12 @@ def tile_picked_zspan_gelu_po_kernel(
                 quantise(codes[n][:, rows], scales[n][:, rows], grouped[n][:, t, :, :].rearrange("p m j -> p (m j)"))
 
         blocks = [slice(b * SPANS, (b + 1) * SPANS) for b in range(BLOCKS)]
-        z_codes = sb("z_codes", [P, S], U32)
-        z_scales = sb("z_scales", [P, S], U8)
-        g_codes = sb("g_codes", [P, S], U32)
-        g_scales = sb("g_scales", [P, S], U8)
+        h_codes = sb("h_codes", [P, 2 * S], U32)
+        h_scales = sb("h_scales", [P, 2 * S], U8)
         o_codes = sb("o_codes", [P, S], I32)
         o_scales = sb("o_scales", [P, S], U8)
         e_vals = {}
-        z_vals = {}
-        g_vals = [sb("g_vals%d" % b, [P, SPANS, PACK], BF16) for b in range(BLOCKS)]
+        h_vals = {}
         o_vals = [sb("o_vals%d" % b, [P, PACK, SPANS], F32) for b in range(BLOCKS)]
         o_round = [sb("o_round%d" % b, [P, SPANS, PACK], BF16) for b in range(BLOCKS)]
         out_rows = out_0.rearrange("(p t) j -> p t j", t=PACK)
@@ -157,21 +161,27 @@ def tile_picked_zspan_gelu_po_kernel(
         def additive(b, bk):
             acc = bank(bk, "g_acc%d" % b)
             product(acc, [(codes[3], scales[3], xs_codes, xs_scales), (codes[4], scales[4], xe_codes, xe_scales)], blocks[b])
-            nc.scalar.activation(out=g_vals[b][:], in_=acc[:].rearrange("p t n -> p n t"), func=GELU)
-            quantise(g_codes[:, blocks[b]], g_scales[:, blocks[b]], g_vals[b][:].rearrange("p n t -> p (n t)"))
+            nc.scalar.activation(out=h_vals[b][:, 1, :, :], in_=acc[:].rearrange("p t n -> p n t"), func=GELU)
+            both = slice(2 * b * SPANS, 2 * (b + 1) * SPANS)
+            quantise(h_codes[:, both], h_scales[:, both], h_vals[b][:].rearrange("p h n t -> p (h n t)"))
 
         def starts(b, bk, tag):
             acc = bank(bk, "y_acc%d" % b)
             product(acc, [(codes[1], scales[1], xs_codes, xs_scales)], blocks[b])
-            z_vals[b] = sb("z_vals%d" % b, [P, SPANS, PACK], BF16, tag)
-            nc.vector.tensor_tensor(z_vals[b][:], acc[:].rearrange("p t n -> p n t"), e_vals[b][:], MULT)
-
-        def quantise_z(b):
-            quantise(z_codes[:, blocks[b]], z_scales[:, blocks[b]], z_vals[b][:].rearrange("p n t -> p (n t)"))
+            h_vals[b] = sb("h_vals%d" % b, [P, 2, SPANS, PACK], BF16, tag)
+            nc.vector.tensor_tensor(h_vals[b][:, 0, :, :], acc[:].rearrange("p t n -> p n t"), e_vals[b][:], MULT)
 
         def labels(b, bk, round_from_psum):
             acc = bank(bk, "o_acc%d" % b)
-            product(acc, [(w5_codes, w56_dealt, z_codes, z_scales), (w6_codes, w56_dealt[4:P, :], g_codes, g_scales)], blocks[b])
+            first = 2 * b * SPANS
+            product(
+                acc,
+                [
+                    (w56_codes[:, 0, :], w56_dealt, h_codes[:, first : first + SPANS], h_scales[:, first : first + SPANS]),
+                    (w56_codes[:, 1, :], w56_dealt[4:P, :], h_codes[:, first + SPANS : first + 2 * SPANS], h_scales[:, first + SPANS : first + 2 * SPANS]),
+                ],
+                slice(0, SPANS),
+            )
             if round_from_psum is not None:
                 round_from_psum(out=o_round[b][:], in_=acc[:].rearrange("p t n -> p n t"))
             nc.scalar.copy(out=o_vals[b][:], in_=acc[:])
@@ -189,31 +199,36 @@ def tile_picked_zspan_gelu_po_kernel(
         w2_codes = deal("w2_codes", w2_raw, I32)
         xs_codes = sb("xs_codes", [P, S], U32, "w2_raw")
         nc.vector.tensor_copy(xs_codes[:], x_table[:].bitcast(U32).indirect(offs_list[:]))
-        nc.scalar.copy(
-            out=grouped[1][:].rearrange("p t m j -> p m j t"), in_=w1_raw[:].rearrange("p j (m t) -> p m j t", t=PACK)
-        )
+        new_weight(1, None, "x_table", "w2_plane")
+        round_cols(nc.scalar.copy, grouped[1], w1_raw, 0, P, 0)
         quantise_weight(1)
-        for h in range(2):
-            round_half(nc.scalar.copy, grouped[3], w3_raw[h], h)
+        ends(0, 0, "w1_raw")
+        new_weight(3)
+        round_cols(nc.scalar.copy, grouped[3], w3_raw, 0, 64, 0)
+        round_cols(nc.vector.tensor_copy, grouped[3], w3_raw, 64, 64, 0)
+        starts(0, BLOCKS, None)
         quantise_weight(3)
-        for b in range(BLOCKS):
-            ends(b, b, "w3_raw1" if b == 0 else None)
-        for h in range(2):
-            round_half(nc.vector.tensor_copy, grouped[4], w4_raw[h], h)
-        quantise_weight_by_tile(4)
+        ends(1, 1, "w3_raw")
+        new_weight(4)
+        round_cols(nc.scalar.copy, grouped[4], w4_raw[0], 0, 64, 0)
+        ends(2, 2, "w4_raw0")
+        ends(3, 3, None)
+        round_cols(nc.vector.tensor_copy, grouped[4], w4_raw[1], 64, 64, 64)
+        quantise_weight(4)
+        w56_codes = sb("w56_codes", [P, 2, N], I32, "w4_grouped")
+        nc.vector.tensor_copy(
+            out=w56_codes[:].rearrange("p w (t m) -> p w m t", t=PACK), in_=w56_raw[:].rearrange("p w (m t) -> p w m t", t=PACK)
+        )
         w56_dealt = deal("w56_dealt", w56_plane, U8)
-        w5_codes = deal("w5_codes", w5_raw, I32)
-        w6_codes = deal("w6_codes", w6_raw, I32)
+        starts(1, BLOCKS + 1, "w56_raw")
+        additive(0, 0)
+        starts(2, BLOCKS + 2, "w56_plane")
+        additive(1, 1)
+        starts(3, BLOCKS + 3, "h_vals0")
+        additive(2, 2)
+        additive(3, 3)
         for b in range(BLOCKS):
-            starts(b, BLOCKS + b, "w4_grouped" if b == 1 else None)
-            if b > 0:
-                quantise_z(b - 1)
-        quantise_z(BLOCKS - 1)
-        rounders = [None, nc.scalar.copy, nc.scalar.copy, nc.vector.tensor_copy]
-        for b in range(BLOCKS):
-            additive(b, b)
-        for b in range(BLOCKS):
-            labels(b, BLOCKS + b, rounders[b])
+            labels(b, BLOCKS + b, None)
             if b > 0:
                 planes(b - 1)
         planes(BLOCKS - 1)

@@ -42,11 +42,8 @@ def tile_picked_zspan_gelu_po_kernel(
             return packed[0].rearrange("p n t -> p (n t)").bitcast(I32)
 
         def load_scale_rows(queue, plane, scales, first):
-            for q in range(QUADS):
-                queue.dma_start(
-                    out=plane[32 * q + first : 32 * q + first + 4, :].bitcast(I32),
-                    in_=scales[0, 4 * q : 4 * q + 4, :].bitcast(I32),
-                )
+            for r in range(4):
+                queue.dma_start(out=plane[first + r : P : 32, :].bitcast(I32), in_=scales[0, r:16:4, :].bitcast(I32))
 
         def load_half(name, w, half):
             raw = sb(name, [P, PACK, HALF], F32)
@@ -96,9 +93,6 @@ def tile_picked_zspan_gelu_po_kernel(
         nc.gpsimd.memset(x_plane[:].bitcast(I32), 0)
         nc.vector.memset(w2_plane[:].bitcast(I32), 0)
         nc.vector.memset(w56_plane[:].bitcast(I32), 0)
-        warm = sb("warm", [P, 2], F32)
-        nc.gpsimd.memset(warm[:, 0:1], 0.0)
-        nc.scalar.activation(out=warm[:, 1:2], in_=warm[:, 0:1], func=GELU)
         end_list = sb("end_list", [P, S // 16], U16)
         offs_list = sb("offs_list", [P, S // 16], U16)
         x_table = sb("x_table", [P, T], I32)
@@ -108,13 +102,13 @@ def tile_picked_zspan_gelu_po_kernel(
         nc.sync.dma_start(offs_list[:], offs)
         load_scale_rows(nc.sync, x_plane, x_scales, 0)
         nc.sync.dma_start(out=x_table[:], in_=as_words(x_words))
-        w1_raw = load_whole("w1_raw", w1)
+        w3_raw = load_whole("w3_raw", w3)
         load_scale_rows(nc.sync, w2_plane, w2_scales, 0)
         nc.sync.dma_start(out=w2_raw[:], in_=as_words(w2_words))
-        w3_raw = load_whole("w3_raw", w3)
-        w4_raw = [load_half("w4_raw0", w4, 0)]
+        w4_raw = load_whole("w4_raw", w4)
+        w1_raw = [load_half("w1_raw0", w1, 0)]
         load_scale_rows(nc.sync, w56_plane, w5_scales, 0)
-        w4_raw.append(load_half("w4_raw1", w4, 1))
+        w1_raw.append(load_half("w1_raw1", w1, 1))
         nc.sync.dma_start(out=w56_raw[:, 0, :], in_=as_words(w5_words))
         nc.sync.dma_start(out=w56_raw[:, 1, :], in_=as_words(w6_words))
         load_scale_rows(nc.sync, w56_plane, w6_scales, 4)
@@ -148,15 +142,14 @@ def tile_picked_zspan_gelu_po_kernel(
         e_vals = {}
         h_vals = {}
         o_vals = [sb("o_vals%d" % b, [P, PACK, SPANS], F32) for b in range(BLOCKS)]
-        o_round = [sb("o_round%d" % b, [P, SPANS, PACK], BF16) for b in range(BLOCKS)]
+        o_round = {}
         out_rows = out_0.rearrange("(p t) j -> p t j", t=PACK)
         out_words = as_words(out_1)
 
-        def ends(b, bk, tag):
+        def ends(b, bk):
             acc = bank(bk, "e_acc%d" % b)
             product(acc, [(w2_codes, w2_dealt, xe_codes, xe_scales)], blocks[b])
-            e_vals[b] = sb("e_vals%d" % b, [P, SPANS, PACK], F32, tag)
-            nc.scalar.copy(out=e_vals[b][:], in_=acc[:].rearrange("p t n -> p n t"))
+            nc.scalar.copy(out=e_vals[b], in_=acc[:].rearrange("p t n -> p n t"))
 
         def additive(b, bk):
             acc = bank(bk, "g_acc%d" % b)
@@ -169,9 +162,9 @@ def tile_picked_zspan_gelu_po_kernel(
             acc = bank(bk, "y_acc%d" % b)
             product(acc, [(codes[1], scales[1], xs_codes, xs_scales)], blocks[b])
             h_vals[b] = sb("h_vals%d" % b, [P, 2, SPANS, PACK], BF16, tag)
-            nc.vector.tensor_tensor(h_vals[b][:, 0, :, :], acc[:].rearrange("p t n -> p n t"), e_vals[b][:], MULT)
+            nc.vector.tensor_tensor(h_vals[b][:, 0, :, :], acc[:].rearrange("p t n -> p n t"), e_vals[b], MULT)
 
-        def labels(b, bk, round_from_psum):
+        def labels(b, bk, round_from_psum, tag):
             acc = bank(bk, "o_acc%d" % b)
             first = 2 * b * SPANS
             product(
@@ -182,6 +175,7 @@ def tile_picked_zspan_gelu_po_kernel(
                 ],
                 slice(0, SPANS),
             )
+            o_round[b] = sb("o_round%d" % b, [P, SPANS, PACK], BF16, tag)
             if round_from_psum is not None:
                 round_from_psum(out=o_round[b][:], in_=acc[:].rearrange("p t n -> p n t"))
             nc.scalar.copy(out=o_vals[b][:], in_=acc[:])
@@ -195,44 +189,46 @@ def tile_picked_zspan_gelu_po_kernel(
         def planes(b):
             quantise(o_codes[:, blocks[b]], o_scales[:, blocks[b]], o_round[b][:].rearrange("p n t -> p (n t)"))
             nc.sync.dma_start(out=out_words[:, blocks[b]], in_=o_codes[:, blocks[b]])
-        w2_dealt = deal("w2_dealt", w2_plane, U8)
-        w2_codes = deal("w2_codes", w2_raw, I32)
-        xs_codes = sb("xs_codes", [P, S], U32, "w2_raw")
+        xs_codes = sb("xs_codes", [P, S], U32)
         nc.vector.tensor_copy(xs_codes[:], x_table[:].bitcast(U32).indirect(offs_list[:]))
-        new_weight(1, None, "x_table", "w2_plane")
-        round_cols(nc.scalar.copy, grouped[1], w1_raw, 0, P, 0)
-        quantise_weight(1)
-        ends(0, 0, "w1_raw")
-        new_weight(3)
-        round_cols(nc.scalar.copy, grouped[3], w3_raw, 0, 64, 0)
-        round_cols(nc.vector.tensor_copy, grouped[3], w3_raw, 64, 64, 0)
-        starts(0, BLOCKS, None)
+        w2_dealt = deal("w2_dealt", w2_plane, U8)
+        w2_codes = deal("w2_codes", w2_raw, I32, "x_table")
+        new_weight(3, None, "w2_raw", "w2_plane")
+        round_cols(nc.scalar.copy, grouped[3], w3_raw, 0, P, 0)
         quantise_weight(3)
-        ends(1, 1, "w3_raw")
         new_weight(4)
-        round_cols(nc.scalar.copy, grouped[4], w4_raw[0], 0, 64, 0)
-        ends(2, 2, "w4_raw0")
-        ends(3, 3, None)
-        round_cols(nc.vector.tensor_copy, grouped[4], w4_raw[1], 64, 64, 64)
+        round_cols(nc.scalar.copy, grouped[4], w4_raw, 0, 64, 0)
+        round_cols(nc.vector.tensor_copy, grouped[4], w4_raw, 64, 64, 0)
         quantise_weight(4)
-        w56_codes = sb("w56_codes", [P, 2, N], I32, "w4_grouped")
+        e_first = sb("e_first", [P, SPANS, PACK], F32, "w4_raw")
+        e_vals[0] = e_first[:]
+        ends(0, 0)
+        new_weight(1)
+        round_cols(nc.scalar.copy, grouped[1], w1_raw[0], 0, 64, 0)
+        round_cols(nc.vector.tensor_copy, grouped[1], w1_raw[1], 64, 64, 64)
+        quantise_weight(1)
+        e_rest = sb("e_rest", [P, BLOCKS - 1, SPANS, PACK], F32, "w1_raw0")
+        for b in range(1, BLOCKS):
+            e_vals[b] = e_rest[:, b - 1, :, :]
+            ends(b, b)
+        w56_codes = sb("w56_codes", [P, 2, N], I32, "w1_grouped")
         nc.vector.tensor_copy(
             out=w56_codes[:].rearrange("p w (t m) -> p w m t", t=PACK), in_=w56_raw[:].rearrange("p w (m t) -> p w m t", t=PACK)
         )
         w56_dealt = deal("w56_dealt", w56_plane, U8)
-        starts(1, BLOCKS + 1, "w56_raw")
-        additive(0, 0)
-        starts(2, BLOCKS + 2, "w56_plane")
-        additive(1, 1)
-        starts(3, BLOCKS + 3, "h_vals0")
-        additive(2, 2)
-        additive(3, 3)
+        starts(0, 6, None)
+        starts(1, 7, None)
+        additive(0, 4)
+        starts(2, 0, None)
+        additive(1, 5)
+        starts(3, 1, None)
+        additive(2, 6)
+        additive(3, 7)
         for b in range(BLOCKS):
-            labels(b, BLOCKS + b, None)
+            labels(b, 2 + b, None, "h_vals%d" % (b + 2) if b < 2 else None)
             if b > 0:
                 planes(b - 1)
         planes(BLOCKS - 1)
-        for q in range(QUADS):
-            nc.sync.dma_start(
-                out=out_2[0, 4 * q : 4 * q + 4, :].bitcast(I32), in_=o_scales[32 * q : 32 * q + 4, :].bitcast(I32)
-            )
+        for r in range(4):
+            queue = nc.sync if r < 2 else nc.scalar
+            queue.dma_start(out=out_2[0, r:16:4, :].bitcast(I32), in_=o_scales[r:P:32, :].bitcast(I32))

@@ -93,6 +93,9 @@ def tile_picked_zspan_gelu_po_kernel(
         nc.gpsimd.memset(x_plane[:].bitcast(I32), 0)
         nc.vector.memset(w2_plane[:].bitcast(I32), 0)
         nc.vector.memset(w56_plane[:].bitcast(I32), 0)
+        warm = sb("warm", [P, 2], F32)
+        nc.gpsimd.memset(warm[:, 0:1], 0.0)
+        nc.scalar.activation(out=warm[:, 1:2], in_=warm[:, 0:1], func=GELU)
         end_list = sb("end_list", [P, S // 16], U16)
         offs_list = sb("offs_list", [P, S // 16], U16)
         x_table = sb("x_table", [P, T], I32)

from contextlib import ExitStack

import concourse.mybir as mybir

K, T, S, H, N = 512, 1024, 512, 512, 512
FLOPS = 2 * S * (4 * K * H + 2 * H * N)

F32 = mybir.dt.float32
BF16 = mybir.dt.bfloat16
I32 = mybir.dt.int32
U32 = mybir.dt.uint32
U16 = mybir.dt.uint16
U8 = mybir.dt.uint8
FP8X4 = mybir.dt.float8_e4m3fn_x4
GELU = mybir.ActivationFunctionType.Gelu_apprx_tanh
MULT = mybir.AluOpType.mult

P = 128
PACK = 4
QUADS = 4
SPANS = 128
BLOCKS = S // SPANS
HALF = H // 2


def tile_picked_zspan_gelu_po_kernel(
    tc, x_words, x_scales, w1, w2_words, w2_scales, w3, w4, w5_words, w5_scales, w6_words, w6_scales, offs, end,
    out_0, out_1, out_2,
):
    nc = tc.nc
    with ExitStack() as ctx:
        keep = ctx.enter_context(tc.tile_pool(name="keep", bufs=1))
        psum = ctx.enter_context(tc.psum_pool(name="psum", bufs=1))

        def sb(name, shape, dtype, tag=None):
            return keep.tile(shape, dtype, name=name, tag=tag or name, align_bytes=64)

        def bank(index, name):
            return psum.tile([P, PACK, SPANS], F32, name=name, tag="bank%d" % index)

        def as_words(packed):
            return packed[0].rearrange("p n t -> p (n t)").bitcast(I32)

        def load_scale_rows(queue, plane, scales, first):
            for r in range(4):
                queue.dma_start(out=plane[first + r : P : 32, :].bitcast(I32), in_=scales[0, r:16:4, :].bitcast(I32))

        def load_half(name, w, half):
            raw = sb(name, [P, PACK, HALF], F32)
            nc.sync.dma_start(
                out=raw[:], in_=w.rearrange("(p j) c -> p j c", j=PACK)[:, :, half * HALF : (half + 1) * HALF]
            )
            return raw

        def load_whole(name, w):
            raw = sb(name, [P, PACK, H], F32)
            nc.sync.dma_start(out=raw[:], in_=w.rearrange("(p j) c -> p j c", j=PACK))
            return raw

        def round_cols(copy, grouped, raw, first, count, base):
            copy(
                out=grouped[:, :, first : first + count, :].rearrange("p t m j -> p m j t"),
                in_=raw[:].rearrange("p j (m t) -> p m j t", t=PACK)[:, first - base : first - base + count, :, :],
            )

        def quantise(codes, scales, values):
            nc.vector.quantize_mx(out=codes.bitcast(FP8X4), scales=scales, in_=values)

        def deal(name, src, dtype, tag=None):
            dealt = sb(name, [P, H], dtype, tag)
            nc.vector.tensor_copy(
                out=dealt[:].rearrange("p (t m) -> p m t", t=PACK), in_=src[:].rearrange("p (m t) -> p m t", t=PACK)
            )
            return dealt

        def product(acc, terms, cols):
            for t in range(PACK):
                rows = slice(t * P, (t + 1) * P)
                for i, (w_codes, w_scales, a_codes, a_scales) in enumerate(terms):
                    nc.tensor.matmul_mx(
                        out=acc[:, t, :],
                        lhsT=w_codes[:, rows].bitcast(FP8X4),
                        lhsT_scale=w_scales[:, rows],
                        rhs=a_codes[:, cols].bitcast(FP8X4),
                        rhs_scale=a_scales[:, cols],
                        start=(i == 0),
                        stop=(i == len(terms) - 1),
                    )

        x_plane = sb("x_plane", [P, T], U8)
        w2_plane = sb("w2_plane", [P, H], U8)
        w56_plane = sb("w56_plane", [P, N], U8)
        nc.gpsimd.memset(x_plane[:].bitcast(I32), 0)
        nc.vector.memset(w2_plane[:].bitcast(I32), 0)
        nc.vector.memset(w56_plane[:].bitcast(I32), 0)
        warm = sb("warm", [P, 2], F32)
        nc.gpsimd.memset(warm[:, 0:1], 0.0)
        nc.scalar.activation(out=warm[:, 1:2], in_=warm[:, 0:1], func=GELU)
        end_list = sb("end_list", [P, S // 16], U16)
        offs_list = sb("offs_list", [P, S // 16], U16)
        x_table = sb("x_table", [P, T], I32)
        w2_raw = sb("w2_raw", [P, H], I32)
        w56_raw = sb("w56_raw", [P, 2, N], I32)
        nc.sync.dma_start(end_list[:], end)
        nc.sync.dma_start(offs_list[:], offs)
        load_scale_rows(nc.sync, x_plane, x_scales, 0)
        nc.sync.dma_start(out=x_table[:], in_=as_words(x_words))
        w3_raw = load_whole("w3_raw", w3)
        load_scale_rows(nc.sync, w2_plane, w2_scales, 0)
        nc.sync.dma_start(out=w2_raw[:], in_=as_words(w2_words))
        w4_raw = load_whole("w4_raw", w4)
        w1_raw = [load_half("w1_raw0", w1, 0)]
        load_scale_rows(nc.sync, w56_plane, w5_scales, 0)
        w1_raw.append(load_half("w1_raw1", w1, 1))
        nc.sync.dma_start(out=w56_raw[:, 0, :], in_=as_words(w5_words))
        nc.sync.dma_start(out=w56_raw[:, 1, :], in_=as_words(w6_words))
        load_scale_rows(nc.sync, w56_plane, w6_scales, 4)
        xe_scales = sb("xe_scales", [P, S], U8)
        xs_scales = sb("xs_scales", [P, S], U8)
        xe_codes = sb("xe_codes", [P, S], U32)
        nc.vector.tensor_copy(xe_scales[:], x_plane[:].indirect(end_list[:]))
        nc.vector.tensor_copy(xs_scales[:], x_plane[:].indirect(offs_list[:]))
        nc.vector.tensor_copy(xe_codes[:], x_table[:].bitcast(U32).indirect(end_list[:]))

        grouped, codes, scales = {}, {}, {}

        def new_weight(n, grouped_tag=None, codes_tag=None, scales_tag=None):
            grouped[n] = sb("w%d_grouped" % n, [P, PACK, P, PACK], BF16, grouped_tag)
            codes[n] = sb("w%d_codes" % n, [P, H], U32, codes_tag)
            scales[n] = sb("w%d_scales_q" % n, [P, H], U8, scales_tag)

        def quantise_weight(n):
            quantise(codes[n][:], scales[n][:], grouped[n][:].rearrange("p t m j -> p (t m j)"))

        def quantise_weight_by_tile(n):
            for t in range(PACK):
                rows = slice(t * P, (t + 1) * P)
                quantise(codes[n][:, rows], scales[n][:, rows], grouped[n][:, t, :, :].rearrange("p m j -> p (m j)"))

        blocks = [slice(b * SPANS, (b + 1) * SPANS) for b in range(BLOCKS)]
        h_codes = sb("h_codes", [P, 2 * S], U32)
        h_scales = sb("h_scales", [P, 2 * S], U8)
        o_codes = sb("o_codes", [P, S], I32)
        o_scales = sb("o_scales", [P, S], U8)
        e_vals = {}
        h_vals = {}
        o_vals = [sb("o_vals%d" % b, [P, PACK, SPANS], F32) for b in range(BLOCKS)]
        o_round = {}
        out_rows = out_0.rearrange("(p t) j -> p t j", t=PACK)
        out_words = as_words(out_1)

        def ends(b, bk):
            acc = bank(bk, "e_acc%d" % b)
            product(acc, [(w2_codes, w2_dealt, xe_codes, xe_scales)], blocks[b])
            nc.scalar.copy(out=e_vals[b], in_=acc[:].rearrange("p t n -> p n t"))

        def additive(b, bk):
            acc = bank(bk, "g_acc%d" % b)
            product(acc, [(codes[3], scales[3], xs_codes, xs_scales), (codes[4], scales[4], xe_codes, xe_scales)], blocks[b])
            nc.scalar.activation(out=h_vals[b][:, 1, :, :], in_=acc[:].rearrange("p t n -> p n t"), func=GELU)
            both = slice(2 * b * SPANS, 2 * (b + 1) * SPANS)
            quantise(h_codes[:, both], h_scales[:, both], h_vals[b][:].rearrange("p h n t -> p (h n t)"))

        def starts(b, bk, tag):
            acc = bank(bk, "y_acc%d" % b)
            product(acc, [(codes[1], scales[1], xs_codes, xs_scales)], blocks[b])
            h_vals[b] = sb("h_vals%d" % b, [P, 2, SPANS, PACK], BF16, tag)
            nc.vector.tensor_tensor(h_vals[b][:, 0, :, :], acc[:].rearrange("p t n -> p n t"), e_vals[b], MULT)

        def labels(b, bk, round_from_psum, tag):
            acc = bank(bk, "o_acc%d" % b)
            first = 2 * b * SPANS
            product(
                acc,
                [
                    (w56_codes[:, 0, :], w56_dealt, h_codes[:, first : first + SPANS], h_scales[:, first : first + SPANS]),
                    (w56_codes[:, 1, :], w56_dealt[4:P, :], h_codes[:, first + SPANS : first + 2 * SPANS], h_scales[:, first + SPANS : first + 2 * SPANS]),
                ],
                slice(0, SPANS),
            )
            o_round[b] = sb("o_round%d" % b, [P, SPANS, PACK], BF16, tag)
            if round_from_psum is not None:
                round_from_psum(out=o_round[b][:], in_=acc[:].rearrange("p t n -> p n t"))
            nc.scalar.copy(out=o_vals[b][:], in_=acc[:])
            nc.sync.dma_start(out=out_rows[:, :, blocks[b]], in_=o_vals[b][:])
            if round_from_psum is None:
                nc.vector.tensor_copy(
                    out=o_round[b][:].rearrange("p (c i) t -> p c t i", i=PACK),
                    in_=o_vals[b][:].rearrange("p t (c i) -> p c t i", i=PACK),
                )

        def planes(b):
            quantise(o_codes[:, blocks[b]], o_scales[:, blocks[b]], o_round[b][:].rearrange("p n t -> p (n t)"))
            nc.sync.dma_start(out=out_words[:, blocks[b]], in_=o_codes[:, blocks[b]])
        xs_codes = sb("xs_codes", [P, S], U32)
        nc.vector.tensor_copy(xs_codes[:], x_table[:].bitcast(U32).indirect(offs_list[:]))
        w2_dealt = deal("w2_dealt", w2_plane, U8)
        w2_codes = deal("w2_codes", w2_raw, I32, "x_table")
        new_weight(3, None, "w2_raw", "w2_plane")
        round_cols(nc.scalar.copy, grouped[3], w3_raw, 0, P, 0)
        quantise_weight(3)
        new_weight(4)
        round_cols(nc.scalar.copy, grouped[4], w4_raw, 0, 64, 0)
        round_cols(nc.vector.tensor_copy, grouped[4], w4_raw, 64, 64, 0)
        quantise_weight(4)
        e_first = sb("e_first", [P, SPANS, PACK], F32, "w4_raw")
        e_vals[0] = e_first[:]
        ends(0, 0)
        new_weight(1)
        round_cols(nc.scalar.copy, grouped[1], w1_raw[0], 0, 64, 0)
        round_cols(nc.vector.tensor_copy, grouped[1], w1_raw[1], 64, 64, 64)
        quantise_weight(1)
        e_rest = sb("e_rest", [P, BLOCKS - 1, SPANS, PACK], F32, "w1_raw0")
        for b in range(1, BLOCKS):
            e_vals[b] = e_rest[:, b - 1, :, :]
            ends(b, b)
        w56_codes = sb("w56_codes", [P, 2, N], I32, "w1_grouped")
        nc.vector.tensor_copy(
            out=w56_codes[:].rearrange("p w (t m) -> p w m t", t=PACK), in_=w56_raw[:].rearrange("p w (m t) -> p w m t", t=PACK)
        )
        w56_dealt = deal("w56_dealt", w56_plane, U8)
        starts(0, 6, None)
        starts(1, 7, None)
        additive(0, 4)
        starts(2, 0, None)
        additive(1, 5)
        starts(3, 1, None)
        additive(2, 6)
        additive(3, 7)
        for b in range(BLOCKS):
            labels(b, 2 + b, None, "h_vals%d" % (b + 2) if b < 2 else None)
            if b > 0:
                planes(b - 1)
        planes(BLOCKS - 1)
        for r in range(4):
            queue = nc.sync if r < 2 else nc.scalar
            queue.dma_start(out=out_2[0, r:16:4, :].bitcast(I32), in_=o_scales[r:P:32, :].bitcast(I32))
